import numpy as np
import ml_dtypes


def mxq(x, axis, fmt="e4m3"):
    dtype, down = {"e4m3": (ml_dtypes.float8_e4m3fn, 7), "e5m2": (ml_dtypes.float8_e5m2, 14)}[fmt]
    v = np.moveaxis(np.asarray(x, np.float32).astype(ml_dtypes.bfloat16).astype(np.float64), axis, -1)
    blocks = v.reshape(v.shape[:-1] + (-1, 32))
    amax = np.abs(blocks).max(-1, keepdims=True)
    byte = np.maximum(np.where(amax > 0, np.frexp(amax)[1] - 1 + 127, 0) - down, 1)
    scale = np.exp2(byte - 127.0)
    codes = (blocks / scale).astype(np.float32).astype(dtype).astype(np.float64)
    return np.moveaxis((codes * scale).reshape(v.shape), -1, axis)


WIDE = False


def mx_kscale(k):
    if not WIDE:
        return np.ones(k)
    levels = np.array([10, -10, 5, -5, 0])
    if k % 512:
        return np.exp2(np.random.permutation(np.resize(levels, k // 32))).repeat(32)
    a = np.empty((k // 512, 16))
    for p in range(k // 512):
        a[p, :8] = np.random.permutation(np.resize(levels, 8))
        for g in range(8):
            far = levels[np.abs(levels - a[p, g]) >= 10]
            a[p, g + 8] = far[np.random.randint(len(far))]
    return np.exp2(a.ravel()).repeat(32)


def f64(x):
    return np.asarray(x).astype(np.float64)


def striped(idx):
    return np.tile(idx.reshape(-1, 16).T, (8, 1)).astype(np.uint16)


def unstriped(offs):
    return offs[:16].T.reshape(-1).astype(np.int64)


def striped8(idx):
    return np.concatenate([x.reshape(-1, 16).T for x in idx]).astype(np.uint16)


def runs(offs, k):
    lists = np.stack([offs[16 * r : 16 * r + 16].T.reshape(-1) for r in range(8)]).astype(np.int64)
    return lists[np.arange(k) % 512 // 64]


def pack_weight(w):
    k, n = w.shape
    w = f64(np.asarray(w, np.float32).astype(ml_dtypes.bfloat16)).reshape(k // 32, 32, n)
    amax = np.abs(w).max(1)
    byte = np.clip(np.where(amax > 0, np.frexp(amax)[1] - 1 + 127 - 7, 1), 1, 254)
    scaled = (w * np.exp2(127.0 - byte)[:, None, :]).reshape(k, n).astype(np.float32)
    words = np.ascontiguousarray(scaled.reshape(k // 512, 128, 4, n).transpose(0, 1, 3, 2)).astype(ml_dtypes.float8_e4m3fn).view(np.uint8)
    return words, np.ascontiguousarray(byte.astype(np.uint8).reshape(k // 512, 16, n))


def unpack_weight(words, scales):
    g, p, n, _ = words.shape
    vals = np.ascontiguousarray(words).view(ml_dtypes.float8_e4m3fn).astype(np.float64) * np.repeat(np.exp2(scales.astype(np.float64) - 127.0), 8, axis=1)[..., None]
    return vals.transpose(0, 1, 3, 2).reshape(g * 512, n)


E2M1 = np.array([0.0, 0.5, 1.0, 1.5, 2.0, 3.0, 4.0, 6.0, -0.0, -0.5, -1.0, -1.5, -2.0, -3.0, -4.0, -6.0])


def pack_fp4(w):
    k, n = w.shape
    w = f64(np.asarray(w, np.float32).astype(ml_dtypes.bfloat16)).reshape(k // 32, 32, n)
    amax = np.abs(w).max(1)
    mant, ex = np.frexp(amax / 6.0)
    byte = np.clip(np.where(amax > 0, np.where(mant > 0.5, ex, ex - 1) + 127, 1), 1, 254)
    scaled = (w * np.exp2(127.0 - byte)[:, None, :]).reshape(k, n).astype(np.float32)
    c = np.ascontiguousarray(scaled.reshape(k // 512, 128, 4, n).transpose(0, 1, 3, 2)).astype(ml_dtypes.float4_e2m1fn).view(np.uint8) & 0xF
    words = (c[..., 0::2] | (c[..., 1::2] << 4)).reshape(k // 512, 128, 2 * n)
    return np.ascontiguousarray(words), np.ascontiguousarray(byte.astype(np.uint8).reshape(k // 512, 16, n))


def unpack_fp4(words, scales):
    g, _, n = scales.shape
    words = np.ascontiguousarray(words).reshape(g, 128, n, 2)
    nib = np.empty((g, 128, n, 4), np.uint8)
    nib[..., 0::2] = words & 0xF
    nib[..., 1::2] = words >> 4
    vals = E2M1[nib] * np.repeat(np.exp2(scales.astype(np.float64) - 127.0), 8, axis=1)[..., None]
    return vals.transpose(0, 1, 3, 2).reshape(g * 512, n)


def planes(y):
    n, m = y.shape
    v = y.astype(np.float32).astype(ml_dtypes.bfloat16).astype(np.float64).reshape(n // 32, 32, m)
    top = np.abs(v).max(1)
    byte = np.clip(np.where(top > 0, np.frexp(top)[1] - 1 + 127 - 7, 1), 1, 254)
    codes = (v * np.exp2(127.0 - byte)[:, None, :]).reshape(n, m).astype(np.float32).astype(ml_dtypes.float8_e4m3fn).view(np.uint8)
    words = codes.reshape(n // 512, 128, 4, m).transpose(0, 1, 3, 2)
    return np.ascontiguousarray(words), np.ascontiguousarray(byte.astype(np.uint8).reshape(n // 512, 16, m))


K, T, S, H, W, C, U = 512, 2048, 512, 512, 256, 512, 1024


def setup_inputs():
    n = np.random.standard_normal
    s = mx_kscale(K)[:, None]
    packed_xT = pack_weight(n((K, T)) * s)
    packed_w1 = pack_fp4(n((K, H)) / np.sqrt(K) / s)
    perm = np.stack([np.random.permutation(S) for _ in range(8)])
    return {
        "x_words": packed_xT[0],
        "x_scales": packed_xT[1],
        "w1_words": packed_w1[0],
        "w1_scales": packed_w1[1],
        "gs": (np.random.uniform(0.5, 1.5, (K, 1)) / s).astype(np.float32),
        "mem": n((C, U)).astype(np.float32),
        "offs": striped(np.random.permutation(T)[:S]),
        "n1": striped8(perm[:, :W]),
        "n2": striped8(perm[:, W:]),
        "n3": striped8(np.stack([np.random.permutation(S) for _ in range(8)])),
        "cand": striped(np.random.permutation(T)[:C]),
        "n4": striped8(np.stack([np.random.permutation(U)[:S] for _ in range(8)])),
        "n5": striped8(np.stack([np.random.permutation(U) for _ in range(8)])),
    }


def reference(x_words, x_scales, w1_words, w1_scales, gs, mem, offs, n1, n2, n3, cand, n4, n5):
    x_cand = unpack_weight(x_words, x_scales)[:, unstriped(cand)]
    xq = unpack_weight(x_words, x_scales)[:, unstriped(offs)]
    y = unpack_fp4(w1_words, w1_scales).T @ xq
    pa = y[np.arange(H)[:, None], runs(n1, H)]
    pb = y[np.arange(H)[:, None], runs(n2, H)]
    ra = pa - (0.5 * pb)
    ds = y.copy()
    ds[np.arange(H)[:, None], runs(n2, H)] = ra
    z = f64(gs) * (ds - (0.5 * (ds[np.arange(H)[:, None], runs(n3, H)])))
    s = 0.0625 * ((x_cand.T @ mxq(z, 0, "e4m3")))
    pg = f64(mem).copy()
    pg[np.arange(C)[:, None], runs(n4, C)] = s
    out_0 = pg - (0.5 * (pg[np.arange(C)[:, None], runs(n5, C)]))
    return (out_0,) + planes(out_0)

@@ -1,0 +1,249 @@
+from contextlib import ExitStack
+
+import concourse.mybir as mybir
+
+F32 = mybir.dt.float32
+BF16 = mybir.dt.bfloat16
+I32 = mybir.dt.int32
+U32 = mybir.dt.uint32
+U16 = mybir.dt.uint16
+U8 = mybir.dt.uint8
+FP8X4 = mybir.dt.float8_e4m3fn_x4
+FP4X4 = mybir.dt.float4_e2m1fn_x4
+ADD = mybir.AluOpType.add
+MULT = mybir.AluOpType.mult
+COPY = mybir.ActivationFunctionType.Copy
+
+P = 128
+PACK = 4
+T = 2048
+S = 512
+U = 1024
+W = 256
+COLS = W // 16
+LAST = PACK - 1
+
+FLOPS = 2 * 2 * 512 * 512 * 512
+
+
+def tile_picked_candfolddpagem_none_po_kernel(
+    tc, x_words, x_scales, w1_words, w1_scales, gs, mem, offs, n1, n2, n3, cand, n4, n5, out_0, out_1, out_2
+):
+    nc = tc.nc
+    with ExitStack() as ctx:
+        held = ctx.enter_context(tc.tile_pool(name="held", bufs=1))
+        psum = ctx.enter_context(tc.psum_pool(name="psum", bufs=1))
+
+        def sb(name, shape, dtype, tag=None):
+            return held.tile([P] + shape, dtype, name=name, tag=tag or name, align_bytes=64)
+
+        def load_list(name, src):
+            tile = held.tile([P, src.shape[1]], U16, name=name)
+            nc.sync.dma_start(tile[:], src)
+            return tile
+
+        def load_scale_rows(queue, tile, src):
+            rows = src[0].bitcast(I32)
+            for q in range(4):
+                queue.dma_start(tile[:].bitcast(I32)[32 * q : 32 * q + 4, :], rows[4 * q : 4 * q + 4, :])
+
+        def piece(lst, i):
+            return lst[:, i * COLS : (i + 1) * COLS]
+
+        xs = sb("xs", [T], U8)
+        ws_raw = sb("ws_raw", [S], U8)
+        nc.vector.memset(xs[:].bitcast(I32), 0)
+        nc.vector.memset(ws_raw[:].bitcast(I32), 0)
+
+        offs_t = load_list("offs_t", offs)
+        cand_t = load_list("cand_t", cand)
+        gs_t = sb("gs_t", [PACK], F32)
+        nc.scalar.dma_start(gs_t[:], gs.rearrange("(p t) o -> p (t o)", t=PACK))
+        ww_raw = sb("ww_raw", [2 * S], U8)
+        nc.scalar.dma_start(ww_raw[:].bitcast(I32), w1_words[0].bitcast(I32))
+        xw = sb("xw", [T], I32)
+        nc.scalar.dma_start(xw[:], x_words[0].rearrange("p n t -> p (n t)").bitcast(I32))
+        load_scale_rows(nc.sync, xs, x_scales)
+        load_scale_rows(nc.scalar, ws_raw, w1_scales)
+        n1_t = load_list("n1_t", n1)
+        n2_t = load_list("n2_t", n2)
+        n3_t = load_list("n3_t", n3)
+        n4_t = load_list("n4_t", n4)
+        n5_t = load_list("n5_t", n5)
+
+        ww = sb("ww", [PACK, 2 * P], U8)
+        nc.vector.tensor_copy(
+            ww[:].rearrange("p t (m b) -> p t m b", b=2),
+            ww_raw[:].rearrange("p (m t b) -> p t m b", t=PACK, b=2),
+        )
+        xq_s = sb("xq_s", [S], U8)
+        nc.vector.tensor_copy(xq_s[:], xs[:].indirect(offs_t[:]))
+        xq_w = sb("xq_w", [S], U32)
+        nc.vector.tensor_copy(xq_w[:], xw[:].bitcast(U32).indirect(offs_t[:]))
+        ws = sb("ws", [PACK, P], U8)
+        nc.vector.tensor_copy(ws[:], ws_raw[:].rearrange("p (m t) -> p t m", t=PACK))
+
+        y_ps = []
+        for t in range(PACK):
+            bank = psum.tile([P, S], F32, name=f"y_ps{t}", tag=f"first{t}")
+            nc.tensor.matmul_mx(
+                out=bank[:],
+                lhsT=ww[:, t, :].bitcast(FP4X4),
+                lhsT_scale=ws[:, t, :],
+                rhs=xq_w[:].bitcast(FP8X4),
+                rhs_scale=xq_s[:],
+                start=True,
+                stop=True,
+            )
+            y_ps.append(bank)
+
+        cw = sb("cw", [PACK, P], U32)
+        nc.vector.tensor_copy(cw[:].rearrange("p t m -> p m t"), xw[:].bitcast(U32).indirect(cand_t[:]))
+        cs = sb("cs", [PACK, P], U8)
+
+        def cand_scales(h, tag):
+            raw = sb(f"cs_raw{h}", [W], U8, tag)
+            nc.vector.tensor_copy(raw[:], xs[:].indirect(piece(cand_t, h)))
+            nc.vector.tensor_copy(cs[:, :, h * P // 2 : (h + 1) * P // 2], raw[:].rearrange("p (m t) -> p t m", t=PACK))
+
+        cand_scales(0, None)
+
+        mem_rows = mem.rearrange("(p t) w -> p t w", t=PACK)
+        pg = [sb(f"pg{t}", [U], F32, tag) for t, tag in enumerate(("ww_raw", "ws_raw", "xw", "xq_w"))]
+        for t in range(PACK):
+            nc.sync.dma_start(pg[t][:], mem_rows[:, t, :])
+
+        u32 = sb("u32", [PACK + 2, W], F32)
+        y_sb = [sb(f"y_sb{t}", [S], F32) for t in range(PACK)]
+        ds = [sb(f"ds{t}", [S], F32) for t in range(PACK)]
+        pa = [sb(f"pa{t}", [W], F32)[:] for t in range(LAST)] + [u32[:, PACK, :]]
+        pb = [sb(f"pb{t}", [W], F32) for t in range(PACK)]
+        twice = [[sb(f"twice{h}_{t}", [W], F32) for t in range(PACK)] for h in range(2)]
+
+        def fetch_pairs(t):
+            nc.scalar.activation(y_sb[t][:], y_ps[t][:], COPY, scale=gs_t[:, t : t + 1])
+            nc.vector.tensor_copy(pa[t], y_sb[t][:].indirect(n1_t[:]))
+            nc.vector.tensor_scalar(pb[t][:], y_sb[t][:].indirect(n2_t[:]), -0.5, 0.0, MULT, ADD)
+
+        def put_pairs(t):
+            nc.scalar.activation(ds[t][:], y_ps[t][:], COPY, scale=gs_t[:, t : t + 1])
+            nc.vector.tensor_tensor(ds[t][:].indirect(n2_t[:]), pa[t], pb[t][:], ADD)
+
+        fetch_pairs(0)
+        for t in range(1, PACK):
+            fetch_pairs(t)
+            put_pairs(t - 1)
+        put_pairs(LAST)
+
+        z16 = [sb(f"z16_{h}", [W, PACK], BF16) for h in range(2)]
+        zw = [sb(f"zw{h}", [W], U32) for h in range(2)]
+        zs = [sb(f"zs{h}", [W], U8) for h in range(2)]
+        sv = [[sb(f"sv{h}_{t}", [W], F32) for t in range(PACK)] for h in range(2)]
+        s_ps = {}
+
+        def double(h, t):
+            nc.scalar.activation(twice[h][t][:], ds[t][:, h * W : (h + 1) * W], COPY, scale=-2.0)
+
+        def fold_z(h, t):
+            nc.vector.tensor_tensor(u32[:, 2 * h + t, :], ds[t][:].indirect(piece(n3_t, h)), twice[h][t][:], ADD)
+
+        def round_z(h):
+            nc.scalar.activation(
+                z16[h][:], u32[:, 2 * h : 2 * h + PACK, :].rearrange("p t c -> p c t"), COPY, scale=-0.5
+            )
+
+        def score(h):
+            nc.vector.quantize_mx(
+                out=zw[h][:].bitcast(FP8X4), scales=zs[h][:], in_=z16[h][:].rearrange("p c t -> p (c t)")
+            )
+            for t in range(PACK):
+                bank = psum.tile([P, W], F32, name=f"s_ps{h}_{t}", tag=("second%d" if h == 0 else "first%d") % t)
+                nc.tensor.matmul_mx(
+                    out=bank[:],
+                    lhsT=cw[:, t, :].bitcast(FP8X4),
+                    lhsT_scale=cs[:, t, :],
+                    rhs=zw[h][:].bitcast(FP8X4),
+                    rhs_scale=zs[h][:],
+                    start=True,
+                    stop=True,
+                )
+                s_ps[h, t] = bank
+
+        def fetch_scores(h, t):
+            nc.scalar.activation(sv[h][t][:], s_ps[h, t][:], COPY, scale=0.0625)
+
+        def put_scores(h, t):
+            nc.vector.tensor_copy(pg[t][:].indirect(piece(n4_t, h)), sv[h][t][:])
+
+        for t in range(LAST):
+            double(0, t)
+            fold_z(0, t)
+            double(1, t)
+        fold_z(1, 2)
+        double(0, LAST)
+        fold_z(0, LAST)
+        double(1, LAST)
+        fold_z(1, LAST)
+        round_z(0)
+        cand_scales(1, f"twice0_{LAST}")
+        score(0)
+        fold_z(1, 0)
+        fold_z(1, 1)
+        fetch_scores(0, 0)
+        fetch_scores(0, 1)
+        round_z(1)
+        put_scores(0, 0)
+        put_scores(0, 1)
+        score(1)
+        for t in range(2, PACK):
+            fetch_scores(0, t)
+            put_scores(0, t)
+        ph = [sb(f"ph{t}", [U], F32) for t in range(PACK)]
+        for t in range(PACK):
+            fetch_scores(1, t)
+        for t in range(PACK):
+            put_scores(1, t)
+            nc.scalar.activation(ph[t][:], pg[t][:], COPY, scale=-0.5)
+
+        out_rows = out_0.rearrange("(p t) w -> p t w", t=PACK)
+        out_words = out_1[0].rearrange("p n t -> p (n t)").bitcast(I32)
+        out_scales = out_2[0].bitcast(I32)
+        chunks = U // W
+        late = sb("o32_late", [2, PACK, W], F32, f"sv1_{LAST}")
+        o32 = [sb("o32_0", [PACK, W], F32)[:], sb("o32_1", [PACK, W], F32, "sv1_2")[:], late[:, 0], late[:, 1]]
+        o16 = [sb(f"o16_{c}", [W, PACK], BF16) for c in range(chunks)]
+        ow = [sb(f"ow{c}", [W], U32) for c in range(chunks)]
+        osc = sb("osc", [U], U8)
+
+        def fold_out(c, t):
+            nc.vector.tensor_tensor(
+                o32[c][:, t, :], ph[t][:].indirect(piece(n5_t, c)), pg[t][:, c * W : (c + 1) * W], ADD
+            )
+
+        def hand_on(c):
+            cols = slice(c * W, (c + 1) * W)
+            nc.vector.quantize_mx(
+                out=ow[c][:].bitcast(FP8X4), scales=osc[:, cols], in_=o16[c][:].rearrange("p c t -> p (c t)")
+            )
+            nc.sync.dma_start(out_words[:, cols], ow[c][:].bitcast(I32))
+
+        for c in range(chunks - 1):
+            for t in range(PACK):
+                fold_out(c, t)
+                if c > 0 and t == PACK - 2:
+                    hand_on(c - 1)
+            nc.sync.dma_start(out_rows[:, :, c * W : (c + 1) * W], o32[c])
+            nc.scalar.copy(o16[c][:], o32[c].rearrange("p t c -> p c t"))
+        c = chunks - 1
+        for t in range(LAST):
+            fold_out(c, t)
+        nc.sync.dma_start(out_rows[:, :LAST, c * W :], o32[c][:, :LAST, :])
+        fold_out(c, LAST)
+        nc.sync.dma_start(out_rows[:, LAST, c * W :], o32[c][:, LAST, :])
+        hand_on(c - 1)
+        nc.scalar.copy(o16[c][:, : W // 2, :], o32[c][:, :, : W // 2].rearrange("p t c -> p c t"))
+        nc.vector.tensor_copy(o16[c][:, W // 2 :, :], o32[c][:, :, W // 2 :].rearrange("p t c -> p c t"))
+        hand_on(c)
+        for q in range(4):
+            queue = nc.scalar if q % 2 == 0 else nc.sync
+            queue.dma_start(out_scales[4 * q : 4 * q + 4, :], osc[:].bitcast(I32)[32 * q : 32 * q + 4, :])

@@ -52,19 +52,22 @@ def tile_picked_candfolddpagem_none_po_kernel(
 
         xs = sb("xs", [T], U8)
         ws_raw = sb("ws_raw", [S], U8)
-        nc.vector.memset(xs[:].bitcast(I32), 0)
+        nc.vector.memset(xs[:, : T // 2].bitcast(I32), 0)
+        nc.gpsimd.memset(xs[:, T // 2 :].bitcast(I32), 0)
         nc.vector.memset(ws_raw[:].bitcast(I32), 0)
 
+        ww_raw = sb("ww_raw", [2 * S], U8)
+        nc.sync.dma_start(ww_raw[:].bitcast(I32), w1_words[0].bitcast(I32))
         offs_t = load_list("offs_t", offs)
+        xw = sb("xw", [T], I32)
+        x_rows = x_words[0].rearrange("p n t -> p (n t)").bitcast(I32)
+        nc.sync.dma_start(xw[:, : T // 2], x_rows[:, : T // 2])
+        load_scale_rows(nc.sync, xs, x_scales)
+        nc.sync.dma_start(xw[:, T // 2 :], x_rows[:, T // 2 :])
+        load_scale_rows(nc.sync, ws_raw, w1_scales)
         cand_t = load_list("cand_t", cand)
         gs_t = sb("gs_t", [PACK], F32)
-        nc.scalar.dma_start(gs_t[:], gs.rearrange("(p t) o -> p (t o)", t=PACK))
-        ww_raw = sb("ww_raw", [2 * S], U8)
-        nc.scalar.dma_start(ww_raw[:].bitcast(I32), w1_words[0].bitcast(I32))
-        xw = sb("xw", [T], I32)
-        nc.scalar.dma_start(xw[:], x_words[0].rearrange("p n t -> p (n t)").bitcast(I32))
-        load_scale_rows(nc.sync, xs, x_scales)
-        load_scale_rows(nc.scalar, ws_raw, w1_scales)
+        nc.sync.dma_start(gs_t[:], gs.rearrange("(p t) o -> p (t o)", t=PACK))
         n1_t = load_list("n1_t", n1)
         n2_t = load_list("n2_t", n2)
         n3_t = load_list("n3_t", n3)
@@ -97,7 +100,7 @@ def tile_picked_candfolddpagem_none_po_kernel(
             )
             y_ps.append(bank)
 
-        cw = sb("cw", [PACK, P], U32)
+        cw = sb("cw", [PACK, P], U32, "ws_raw")
         nc.vector.tensor_copy(cw[:].rearrange("p t m -> p m t"), xw[:].bitcast(U32).indirect(cand_t[:]))
         cs = sb("cs", [PACK, P], U8)
 
@@ -109,7 +112,7 @@ def tile_picked_candfolddpagem_none_po_kernel(
         cand_scales(0, None)
 
         mem_rows = mem.rearrange("(p t) w -> p t w", t=PACK)
-        pg = [sb(f"pg{t}", [U], F32, tag) for t, tag in enumerate(("ww_raw", "ws_raw", "xw", "xq_w"))]
+        pg = [sb(f"pg{t}", [U], F32, tag) for t, tag in enumerate(("ww", "xq_s", "xq_w", "xw"))]
         for t in range(PACK):
             nc.sync.dma_start(pg[t][:], mem_rows[:, t, :])
 
@@ -209,8 +212,8 @@ def tile_picked_candfolddpagem_none_po_kernel(
         out_words = out_1[0].rearrange("p n t -> p (n t)").bitcast(I32)
         out_scales = out_2[0].bitcast(I32)
         chunks = U // W
-        late = sb("o32_late", [2, PACK, W], F32, f"sv1_{LAST}")
-        o32 = [sb("o32_0", [PACK, W], F32)[:], sb("o32_1", [PACK, W], F32, "sv1_2")[:], late[:, 0], late[:, 1]]
+        middle = sb("o32_middle", [2, PACK, W], F32, f"sv1_{LAST}")
+        o32 = [sb("o32_0", [PACK, W], F32)[:], middle[:, 0], middle[:, 1]]
         o16 = [sb(f"o16_{c}", [W, PACK], BF16) for c in range(chunks)]
         ow = [sb(f"ow{c}", [W], U32) for c in range(chunks)]
         osc = sb("osc", [U], U8)
@@ -235,14 +238,15 @@ def tile_picked_candfolddpagem_none_po_kernel(
             nc.sync.dma_start(out_rows[:, :, c * W : (c + 1) * W], o32[c])
             nc.scalar.copy(o16[c][:], o32[c].rearrange("p t c -> p c t"))
         c = chunks - 1
+        o32.append(sb("o32_last", [PACK, W], F32, "o16_0")[:])
         for t in range(LAST):
             fold_out(c, t)
         nc.sync.dma_start(out_rows[:, :LAST, c * W :], o32[c][:, :LAST, :])
         fold_out(c, LAST)
         nc.sync.dma_start(out_rows[:, LAST, c * W :], o32[c][:, LAST, :])
         hand_on(c - 1)
-        nc.scalar.copy(o16[c][:, : W // 2, :], o32[c][:, :, : W // 2].rearrange("p t c -> p c t"))
-        nc.vector.tensor_copy(o16[c][:, W // 2 :, :], o32[c][:, :, W // 2 :].rearrange("p t c -> p c t"))
+        nc.scalar.copy(o16[c][:, : W // 4, :], o32[c][:, :, : W // 4].rearrange("p t c -> p c t"))
+        nc.vector.tensor_copy(o16[c][:, W // 4 :, :], o32[c][:, :, W // 4 :].rearrange("p t c -> p c t"))
         hand_on(c)
         for q in range(4):
             queue = nc.scalar if q % 2 == 0 else nc.sync

@@ -100,16 +100,10 @@ def tile_picked_candfolddpagem_none_po_kernel(
             )
             y_ps.append(bank)
 
-        cw = sb("cw", [PACK, P], U32, "ws_raw")
-        nc.vector.tensor_copy(cw[:].rearrange("p t m -> p m t"), xw[:].bitcast(U32).indirect(cand_t[:]))
-        cs = sb("cs", [PACK, P], U8)
-
-        def cand_scales(h, tag):
-            raw = sb(f"cs_raw{h}", [W], U8, tag)
-            nc.vector.tensor_copy(raw[:], xs[:].indirect(piece(cand_t, h)))
-            nc.vector.tensor_copy(cs[:, :, h * P // 2 : (h + 1) * P // 2], raw[:].rearrange("p (m t) -> p t m", t=PACK))
-
-        cand_scales(0, None)
+        cs_raw = sb("cs_raw", [S], U8)
+        nc.vector.tensor_copy(cs_raw[:], xs[:].indirect(cand_t[:]))
+        cw_raw = sb("cw_raw", [S], U32)
+        nc.vector.tensor_copy(cw_raw[:], xw[:].bitcast(U32).indirect(cand_t[:]))
 
         mem_rows = mem.rearrange("(p t) w -> p t w", t=PACK)
         pg = [sb(f"pg{t}", [U], F32, tag) for t, tag in enumerate(("ww", "xq_s", "xq_w", "xw"))]
@@ -119,7 +113,7 @@ def tile_picked_candfolddpagem_none_po_kernel(
         u32 = sb("u32", [PACK + 2, W], F32)
         y_sb = [sb(f"y_sb{t}", [S], F32) for t in range(PACK)]
         ds = [sb(f"ds{t}", [S], F32) for t in range(PACK)]
-        pa = [sb(f"pa{t}", [W], F32)[:] for t in range(LAST)] + [u32[:, PACK, :]]
+        pa = [sb(f"pa{t}", [W], F32)[:] for t in range(PACK)]
         pb = [sb(f"pb{t}", [W], F32) for t in range(PACK)]
         twice = [[sb(f"twice{h}_{t}", [W], F32) for t in range(PACK)] for h in range(2)]
 
@@ -148,11 +142,11 @@ def tile_picked_candfolddpagem_none_po_kernel(
             nc.scalar.activation(twice[h][t][:], ds[t][:, h * W : (h + 1) * W], COPY, scale=-2.0)
 
         def fold_z(h, t):
-            nc.vector.tensor_tensor(u32[:, 2 * h + t, :], ds[t][:].indirect(piece(n3_t, h)), twice[h][t][:], ADD)
+            nc.vector.tensor_tensor(u32[:, 2 - 2 * h + t, :], ds[t][:].indirect(piece(n3_t, h)), twice[h][t][:], ADD)
 
         def round_z(h):
             nc.scalar.activation(
-                z16[h][:], u32[:, 2 * h : 2 * h + PACK, :].rearrange("p t c -> p c t"), COPY, scale=-0.5
+                z16[h][:], u32[:, 2 - 2 * h : 2 - 2 * h + PACK, :].rearrange("p t c -> p c t"), COPY, scale=-0.5
             )
 
         def score(h):
@@ -178,20 +172,24 @@ def tile_picked_candfolddpagem_none_po_kernel(
         def put_scores(h, t):
             nc.vector.tensor_copy(pg[t][:].indirect(piece(n4_t, h)), sv[h][t][:])
 
-        for t in range(LAST):
+        for t in range(PACK):
             double(0, t)
             fold_z(0, t)
+        for t in range(PACK):
             double(1, t)
-        fold_z(1, 2)
-        double(0, LAST)
-        fold_z(0, LAST)
-        double(1, LAST)
-        fold_z(1, LAST)
-        round_z(0)
-        cand_scales(1, f"twice0_{LAST}")
-        score(0)
         fold_z(1, 0)
         fold_z(1, 1)
+        round_z(0)
+        cs = sb("cs", [PACK, P], U8, f"twice0_{LAST}")
+        nc.vector.tensor_copy(cs[:], cs_raw[:].rearrange("p (m t) -> p t m", t=PACK))
+        cw = sb("cw", [PACK, P], U32, "twice1_0")
+        nc.vector.tensor_copy(
+            cw[:].rearrange("p t (a i) -> p a t i", i=PACK),
+            cw_raw[:].rearrange("p (a i t) -> p a t i", i=PACK, t=PACK),
+        )
+        score(0)
+        fold_z(1, 2)
+        fold_z(1, 3)
         fetch_scores(0, 0)
         fetch_scores(0, 1)
         round_z(1)
@@ -204,16 +202,18 @@ def tile_picked_candfolddpagem_none_po_kernel(
         ph = [sb(f"ph{t}", [U], F32) for t in range(PACK)]
         for t in range(PACK):
             fetch_scores(1, t)
+        minus_half = sb("minus_half", [1], F32)
+        nc.gpsimd.memset(minus_half[:], -0.5)
         for t in range(PACK):
             put_scores(1, t)
-            nc.scalar.activation(ph[t][:], pg[t][:], COPY, scale=-0.5)
+            nc.scalar.activation(ph[t][:], pg[t][:], COPY, scale=minus_half[:])
 
         out_rows = out_0.rearrange("(p t) w -> p t w", t=PACK)
         out_words = out_1[0].rearrange("p n t -> p (n t)").bitcast(I32)
         out_scales = out_2[0].bitcast(I32)
         chunks = U // W
-        middle = sb("o32_middle", [2, PACK, W], F32, f"sv1_{LAST}")
-        o32 = [sb("o32_0", [PACK, W], F32)[:], middle[:, 0], middle[:, 1]]
+        later = sb("o32_later", [chunks - 1, PACK, W], F32, "minus_half")
+        o32 = [sb("o32_0", [PACK, W], F32)[:]] + [later[:, c] for c in range(chunks - 1)]
         o16 = [sb(f"o16_{c}", [W, PACK], BF16) for c in range(chunks)]
         ow = [sb(f"ow{c}", [W], U32) for c in range(chunks)]
         osc = sb("osc", [U], U8)
@@ -238,7 +238,6 @@ def tile_picked_candfolddpagem_none_po_kernel(
             nc.sync.dma_start(out_rows[:, :, c * W : (c + 1) * W], o32[c])
             nc.scalar.copy(o16[c][:], o32[c].rearrange("p t c -> p c t"))
         c = chunks - 1
-        o32.append(sb("o32_last", [PACK, W], F32, "o16_0")[:])
         for t in range(LAST):
             fold_out(c, t)
         nc.sync.dma_start(out_rows[:, :LAST, c * W :], o32[c][:, :LAST, :])

@@ -42,9 +42,9 @@ def tile_picked_candfolddpagem_none_po_kernel(
             nc.sync.dma_start(tile[:], src)
             return tile
 
-        def load_scale_rows(queue, tile, src):
+        def load_scale_rows(queues, tile, src):
             rows = src[0].bitcast(I32)
-            for q in range(4):
+            for q, queue in enumerate(queues):
                 queue.dma_start(tile[:].bitcast(I32)[32 * q : 32 * q + 4, :], rows[4 * q : 4 * q + 4, :])
 
         def piece(lst, i):
@@ -54,7 +54,7 @@ def tile_picked_candfolddpagem_none_po_kernel(
         ws_raw = sb("ws_raw", [S], U8)
         nc.vector.memset(xs[:, : T // 2].bitcast(I32), 0)
         nc.gpsimd.memset(xs[:, T // 2 :].bitcast(I32), 0)
-        nc.vector.memset(ws_raw[:].bitcast(I32), 0)
+        nc.gpsimd.memset(ws_raw[:].bitcast(I32), 0)
 
         ww_raw = sb("ww_raw", [2 * S], U8)
         nc.sync.dma_start(ww_raw[:].bitcast(I32), w1_words[0].bitcast(I32))
@@ -62,9 +62,9 @@ def tile_picked_candfolddpagem_none_po_kernel(
         xw = sb("xw", [T], I32)
         x_rows = x_words[0].rearrange("p n t -> p (n t)").bitcast(I32)
         nc.sync.dma_start(xw[:, : T // 2], x_rows[:, : T // 2])
-        load_scale_rows(nc.sync, xs, x_scales)
+        load_scale_rows([nc.sync] * 4, xs, x_scales)
         nc.sync.dma_start(xw[:, T // 2 :], x_rows[:, T // 2 :])
-        load_scale_rows(nc.sync, ws_raw, w1_scales)
+        load_scale_rows([nc.gpsimd] * 2 + [nc.sync] * 2, ws_raw, w1_scales)
         cand_t = load_list("cand_t", cand)
         gs_t = sb("gs_t", [PACK], F32)
         nc.sync.dma_start(gs_t[:], gs.rearrange("(p t) o -> p (t o)", t=PACK))
@@ -84,7 +84,7 @@ def tile_picked_candfolddpagem_none_po_kernel(
         xq_w = sb("xq_w", [S], U32)
         nc.vector.tensor_copy(xq_w[:], xw[:].bitcast(U32).indirect(offs_t[:]))
         ws = sb("ws", [PACK, P], U8)
-        nc.vector.tensor_copy(ws[:], ws_raw[:].rearrange("p (m t) -> p t m", t=PACK))
+        nc.gpsimd.tensor_copy(ws[:], ws_raw[:].rearrange("p (m t) -> p t m", t=PACK))
 
         y_ps = []
         for t in range(PACK):
@@ -203,7 +203,7 @@ def tile_picked_candfolddpagem_none_po_kernel(
         for t in range(PACK):
             fetch_scores(1, t)
         minus_half = sb("minus_half", [1], F32)
-        nc.gpsimd.memset(minus_half[:], -0.5)
+        nc.vector.memset(minus_half[:], -0.5)
         for t in range(PACK):
             put_scores(1, t)
             nc.scalar.activation(ph[t][:], pg[t][:], COPY, scale=minus_half[:])

@@ -132,11 +132,9 @@ def tile_picked_candfolddpagem_none_po_kernel(
             put_pairs(t - 1)
         put_pairs(LAST)
 
-        z16 = [sb(f"z16_{h}", [W, PACK], BF16) for h in range(2)]
-        zw = [sb(f"zw{h}", [W], U32) for h in range(2)]
-        zs = [sb(f"zs{h}", [W], U8) for h in range(2)]
-        sv = [[sb(f"sv{h}_{t}", [W], F32) for t in range(PACK)] for h in range(2)]
-        s_ps = {}
+        z16 = sb("z16", [S, PACK], BF16)
+        zw = sb("zw", [S], U32)
+        zs = sb("zs", [S], U8)
 
         def double(h, t):
             nc.scalar.activation(twice[h][t][:], ds[t][:, h * W : (h + 1) * W], COPY, scale=-2.0)
@@ -144,33 +142,30 @@ def tile_picked_candfolddpagem_none_po_kernel(
         def fold_z(h, t):
             nc.vector.tensor_tensor(u32[:, 2 - 2 * h + t, :], ds[t][:].indirect(piece(n3_t, h)), twice[h][t][:], ADD)
 
-        def round_z(h):
-            nc.scalar.activation(
-                z16[h][:], u32[:, 2 - 2 * h : 2 - 2 * h + PACK, :].rearrange("p t c -> p c t"), COPY, scale=-0.5
-            )
+        def round_z(a, b):
+            h = a // W
+            planes = u32[:, 2 - 2 * h : 2 - 2 * h + PACK, a - h * W : b - h * W]
+            nc.scalar.activation(z16[:, a:b, :], planes.rearrange("p t c -> p c t"), COPY, scale=-0.5)
 
-        def score(h):
+        def quantise_z(a, b):
             nc.vector.quantize_mx(
-                out=zw[h][:].bitcast(FP8X4), scales=zs[h][:], in_=z16[h][:].rearrange("p c t -> p (c t)")
+                out=zw[:, a:b].bitcast(FP8X4), scales=zs[:, a:b], in_=z16[:, a:b, :].rearrange("p c t -> p (c t)")
             )
-            for t in range(PACK):
-                bank = psum.tile([P, W], F32, name=f"s_ps{h}_{t}", tag=("second%d" if h == 0 else "first%d") % t)
-                nc.tensor.matmul_mx(
-                    out=bank[:],
-                    lhsT=cw[:, t, :].bitcast(FP8X4),
-                    lhsT_scale=cs[:, t, :],
-                    rhs=zw[h][:].bitcast(FP8X4),
-                    rhs_scale=zs[h][:],
-                    start=True,
-                    stop=True,
-                )
-                s_ps[h, t] = bank
 
-        def fetch_scores(h, t):
-            nc.scalar.activation(sv[h][t][:], s_ps[h, t][:], COPY, scale=0.0625)
-
-        def put_scores(h, t):
-            nc.vector.tensor_copy(pg[t][:].indirect(piece(n4_t, h)), sv[h][t][:])
+        def score(t, a, b, bank_tag):
+            bank = psum.tile([P, b - a], F32, name=f"s_ps{t}_{a}", tag=bank_tag)
+            nc.tensor.matmul_mx(
+                out=bank[:],
+                lhsT=cw[:, t, :].bitcast(FP8X4),
+                lhsT_scale=cs[:, t, :],
+                rhs=zw[:, a:b].bitcast(FP8X4),
+                rhs_scale=zs[:, a:b],
+                start=True,
+                stop=True,
+            )
+            scores = sb(f"s{t}_{a}", [b - a], F32)
+            nc.scalar.activation(scores[:], bank[:], COPY, scale=0.0625)
+            nc.vector.tensor_copy(pg[t][:].indirect(n4_t[:, a // 16 : b // 16]), scores[:])
 
         for t in range(PACK):
             double(0, t)
@@ -179,7 +174,8 @@ def tile_picked_candfolddpagem_none_po_kernel(
             double(1, t)
         fold_z(1, 0)
         fold_z(1, 1)
-        round_z(0)
+        round_z(0, P)
+        round_z(P, W)
         cs = sb("cs", [PACK, P], U8, f"twice0_{LAST}")
         nc.vector.tensor_copy(cs[:], cs_raw[:].rearrange("p (m t) -> p t m", t=PACK))
         cw = sb("cw", [PACK, P], U32, "twice1_0")
@@ -187,25 +183,23 @@ def tile_picked_candfolddpagem_none_po_kernel(
             cw[:].rearrange("p t (a i) -> p a t i", i=PACK),
             cw_raw[:].rearrange("p (a i t) -> p a t i", i=PACK, t=PACK),
         )
-        score(0)
+        quantise_z(0, P)
+        quantise_z(P, W)
         fold_z(1, 2)
         fold_z(1, 3)
-        fetch_scores(0, 0)
-        fetch_scores(0, 1)
-        round_z(1)
-        put_scores(0, 0)
-        put_scores(0, 1)
-        score(1)
+        score(0, 0, P, "second0")
+        score(1, 0, W, "second1")
+        score(0, P, W, "first0")
+        round_z(W, S)
+        quantise_z(W, S)
         for t in range(2, PACK):
-            fetch_scores(0, t)
-            put_scores(0, t)
-        ph = [sb(f"ph{t}", [U], F32) for t in range(PACK)]
+            score(t, 0, W, f"second{t}")
         for t in range(PACK):
-            fetch_scores(1, t)
+            score(t, W, S, f"first{t}")
+        ph = [sb(f"ph{t}", [U], F32) for t in range(PACK)]
         minus_half = sb("minus_half", [1], F32)
         nc.vector.memset(minus_half[:], -0.5)
         for t in range(PACK):
-            put_scores(1, t)
             nc.scalar.activation(ph[t][:], pg[t][:], COPY, scale=minus_half[:])
 
         out_rows = out_0.rearrange("(p t) w -> p t w", t=PACK)
@@ -244,9 +238,17 @@ def tile_picked_candfolddpagem_none_po_kernel(
         fold_out(c, LAST)
         nc.sync.dma_start(out_rows[:, LAST, c * W :], o32[c][:, LAST, :])
         hand_on(c - 1)
-        nc.scalar.copy(o16[c][:, : W // 4, :], o32[c][:, :, : W // 4].rearrange("p t c -> p c t"))
-        nc.vector.tensor_copy(o16[c][:, W // 4 :, :], o32[c][:, :, W // 4 :].rearrange("p t c -> p c t"))
-        hand_on(c)
+        planes = o32[c].rearrange("p t c -> p c t")
+        nc.scalar.copy(o16[c][:, : W // 4, :], planes[:, : W // 4, :])
+        nc.vector.tensor_copy(o16[c][:, W // 2 :, :], planes[:, W // 2 :, :])
+        nc.vector.tensor_copy(o16[c][:, W // 4 : W // 2, :], planes[:, W // 4 : W // 2, :])
+        for a in (W // 2, 0):
+            nc.vector.quantize_mx(
+                out=ow[c][:, a : a + P].bitcast(FP8X4),
+                scales=osc[:, c * W + a : c * W + a + P],
+                in_=o16[c][:, a : a + P, :].rearrange("p c t -> p (c t)"),
+            )
+        nc.sync.dma_start(out_words[:, c * W :], ow[c][:].bitcast(I32))
         for q in range(4):
             queue = nc.scalar if q % 2 == 0 else nc.sync
             queue.dma_start(out_scales[4 * q : 4 * q + 4, :], osc[:].bitcast(I32)[32 * q : 32 * q + 4, :])

from contextlib import ExitStack

import concourse.mybir as mybir

F32 = mybir.dt.float32
BF16 = mybir.dt.bfloat16
I32 = mybir.dt.int32
U32 = mybir.dt.uint32
U16 = mybir.dt.uint16
U8 = mybir.dt.uint8
FP8X4 = mybir.dt.float8_e4m3fn_x4
FP4X4 = mybir.dt.float4_e2m1fn_x4
ADD = mybir.AluOpType.add
MULT = mybir.AluOpType.mult
COPY = mybir.ActivationFunctionType.Copy

P = 128
PACK = 4
T = 2048
S = 512
U = 1024
W = 256
COLS = W // 16
LAST = PACK - 1

FLOPS = 2 * 2 * 512 * 512 * 512


def tile_picked_candfolddpagem_none_po_kernel(
    tc, x_words, x_scales, w1_words, w1_scales, gs, mem, offs, n1, n2, n3, cand, n4, n5, out_0, out_1, out_2
):
    nc = tc.nc
    with ExitStack() as ctx:
        held = ctx.enter_context(tc.tile_pool(name="held", bufs=1))
        psum = ctx.enter_context(tc.psum_pool(name="psum", bufs=1))

        def sb(name, shape, dtype, tag=None):
            return held.tile([P] + shape, dtype, name=name, tag=tag or name, align_bytes=64)

        def load_list(name, src):
            tile = held.tile([P, src.shape[1]], U16, name=name)
            nc.sync.dma_start(tile[:], src)
            return tile

        def load_scale_rows(queues, tile, src):
            rows = src[0].bitcast(I32)
            for q, queue in enumerate(queues):
                queue.dma_start(tile[:].bitcast(I32)[32 * q : 32 * q + 4, :], rows[4 * q : 4 * q + 4, :])

        def piece(lst, i):
            return lst[:, i * COLS : (i + 1) * COLS]

        xs = sb("xs", [T], U8)
        ws_raw = sb("ws_raw", [S], U8)
        nc.vector.memset(xs[:, : T // 2].bitcast(I32), 0)
        nc.gpsimd.memset(xs[:, T // 2 :].bitcast(I32), 0)
        nc.gpsimd.memset(ws_raw[:].bitcast(I32), 0)

        ww_raw = sb("ww_raw", [2 * S], U8)
        nc.sync.dma_start(ww_raw[:].bitcast(I32), w1_words[0].bitcast(I32))
        offs_t = load_list("offs_t", offs)
        xw = sb("xw", [T], I32)
        x_rows = x_words[0].rearrange("p n t -> p (n t)").bitcast(I32)
        nc.sync.dma_start(xw[:, : T // 2], x_rows[:, : T // 2])
        load_scale_rows([nc.sync] * 4, xs, x_scales)
        nc.sync.dma_start(xw[:, T // 2 :], x_rows[:, T // 2 :])
        load_scale_rows([nc.gpsimd] * 2 + [nc.sync] * 2, ws_raw, w1_scales)
        cand_t = load_list("cand_t", cand)
        gs_t = sb("gs_t", [PACK], F32)
        nc.sync.dma_start(gs_t[:], gs.rearrange("(p t) o -> p (t o)", t=PACK))
        n1_t = load_list("n1_t", n1)
        n2_t = load_list("n2_t", n2)
        n3_t = load_list("n3_t", n3)
        n4_t = load_list("n4_t", n4)
        n5_t = load_list("n5_t", n5)

        ww = sb("ww", [PACK, 2 * P], U8)
        nc.vector.tensor_copy(
            ww[:].rearrange("p t (m b) -> p t m b", b=2),
            ww_raw[:].rearrange("p (m t b) -> p t m b", t=PACK, b=2),
        )
        xq_s = sb("xq_s", [S], U8)
        nc.vector.tensor_copy(xq_s[:], xs[:].indirect(offs_t[:]))
        xq_w = sb("xq_w", [S], U32)
        nc.vector.tensor_copy(xq_w[:], xw[:].bitcast(U32).indirect(offs_t[:]))
        ws = sb("ws", [PACK, P], U8)
        nc.gpsimd.tensor_copy(ws[:], ws_raw[:].rearrange("p (m t) -> p t m", t=PACK))

        y_ps = []
        for t in range(PACK):
            bank = psum.tile([P, S], F32, name=f"y_ps{t}", tag=f"first{t}")
            nc.tensor.matmul_mx(
                out=bank[:],
                lhsT=ww[:, t, :].bitcast(FP4X4),
                lhsT_scale=ws[:, t, :],
                rhs=xq_w[:].bitcast(FP8X4),
                rhs_scale=xq_s[:],
                start=True,
                stop=True,
            )
            y_ps.append(bank)

        cs_raw = sb("cs_raw", [S], U8)
        nc.vector.tensor_copy(cs_raw[:], xs[:].indirect(cand_t[:]))
        cw_raw = sb("cw_raw", [S], U32)
        nc.vector.tensor_copy(cw_raw[:], xw[:].bitcast(U32).indirect(cand_t[:]))

        mem_rows = mem.rearrange("(p t) w -> p t w", t=PACK)
        pg = [sb(f"pg{t}", [U], F32, tag) for t, tag in enumerate(("ww", "xq_s", "xq_w", "xw"))]
        for t in range(PACK):
            nc.sync.dma_start(pg[t][:], mem_rows[:, t, :])

        u32 = sb("u32", [PACK + 2, W], F32)
        y_sb = [sb(f"y_sb{t}", [S], F32) for t in range(PACK)]
        ds = [sb(f"ds{t}", [S], F32) for t in range(PACK)]
        pa = [sb(f"pa{t}", [W], F32)[:] for t in range(PACK)]
        pb = [sb(f"pb{t}", [W], F32) for t in range(PACK)]
        twice = [[sb(f"twice{h}_{t}", [W], F32) for t in range(PACK)] for h in range(2)]

        def fetch_pairs(t):
            nc.scalar.activation(y_sb[t][:], y_ps[t][:], COPY, scale=gs_t[:, t : t + 1])
            nc.vector.tensor_copy(pa[t], y_sb[t][:].indirect(n1_t[:]))
            nc.vector.tensor_scalar(pb[t][:], y_sb[t][:].indirect(n2_t[:]), -0.5, 0.0, MULT, ADD)

        def put_pairs(t):
            nc.scalar.activation(ds[t][:], y_ps[t][:], COPY, scale=gs_t[:, t : t + 1])
            nc.vector.tensor_tensor(ds[t][:].indirect(n2_t[:]), pa[t], pb[t][:], ADD)

        fetch_pairs(0)
        for t in range(1, PACK):
            fetch_pairs(t)
            put_pairs(t - 1)
        put_pairs(LAST)

        z16 = sb("z16", [S, PACK], BF16)
        zw = sb("zw", [S], U32)
        zs = sb("zs", [S], U8)

        def double(h, t):
            nc.scalar.activation(twice[h][t][:], ds[t][:, h * W : (h + 1) * W], COPY, scale=-2.0)

        def fold_z(h, t):
            nc.vector.tensor_tensor(u32[:, 2 - 2 * h + t, :], ds[t][:].indirect(piece(n3_t, h)), twice[h][t][:], ADD)

        def round_z(a, b):
            h = a // W
            planes = u32[:, 2 - 2 * h : 2 - 2 * h + PACK, a - h * W : b - h * W]
            nc.scalar.activation(z16[:, a:b, :], planes.rearrange("p t c -> p c t"), COPY, scale=-0.5)

        def quantise_z(a, b):
            nc.vector.quantize_mx(
                out=zw[:, a:b].bitcast(FP8X4), scales=zs[:, a:b], in_=z16[:, a:b, :].rearrange("p c t -> p (c t)")
            )

        def score(t, a, b, bank_tag):
            bank = psum.tile([P, b - a], F32, name=f"s_ps{t}_{a}", tag=bank_tag)
            nc.tensor.matmul_mx(
                out=bank[:],
                lhsT=cw[:, t, :].bitcast(FP8X4),
                lhsT_scale=cs[:, t, :],
                rhs=zw[:, a:b].bitcast(FP8X4),
                rhs_scale=zs[:, a:b],
                start=True,
                stop=True,
            )
            scores = sb(f"s{t}_{a}", [b - a], F32)
            nc.scalar.activation(scores[:], bank[:], COPY, scale=0.0625)
            nc.vector.tensor_copy(pg[t][:].indirect(n4_t[:, a // 16 : b // 16]), scores[:])

        for t in range(PACK):
            double(0, t)
            fold_z(0, t)
        for t in range(PACK):
            double(1, t)
        fold_z(1, 0)
        fold_z(1, 1)
        round_z(0, P)
        round_z(P, W)
        cs = sb("cs", [PACK, P], U8, f"twice0_{LAST}")
        nc.vector.tensor_copy(cs[:], cs_raw[:].rearrange("p (m t) -> p t m", t=PACK))
        cw = sb("cw", [PACK, P], U32, "twice1_0")
        nc.vector.tensor_copy(
            cw[:].rearrange("p t (a i) -> p a t i", i=PACK),
            cw_raw[:].rearrange("p (a i t) -> p a t i", i=PACK, t=PACK),
        )
        quantise_z(0, P)
        quantise_z(P, W)
        fold_z(1, 2)
        fold_z(1, 3)
        score(0, 0, P, "second0")
        score(1, 0, W, "second1")
        score(0, P, W, "first0")
        round_z(W, S)
        quantise_z(W, S)
        for t in range(2, PACK):
            score(t, 0, W, f"second{t}")
        for t in range(PACK):
            score(t, W, S, f"first{t}")
        ph = [sb(f"ph{t}", [U], F32) for t in range(PACK)]
        minus_half = sb("minus_half", [1], F32)
        nc.vector.memset(minus_half[:], -0.5)
        for t in range(PACK):
            nc.scalar.activation(ph[t][:], pg[t][:], COPY, scale=minus_half[:])

        out_rows = out_0.rearrange("(p t) w -> p t w", t=PACK)
        out_words = out_1[0].rearrange("p n t -> p (n t)").bitcast(I32)
        out_scales = out_2[0].bitcast(I32)
        chunks = U // W
        later = sb("o32_later", [chunks - 1, PACK, W], F32, "minus_half")
        o32 = [sb("o32_0", [PACK, W], F32)[:]] + [later[:, c] for c in range(chunks - 1)]
        o16 = [sb(f"o16_{c}", [W, PACK], BF16) for c in range(chunks)]
        ow = [sb(f"ow{c}", [W], U32) for c in range(chunks)]
        osc = sb("osc", [U], U8)

        def fold_out(c, t):
            nc.vector.tensor_tensor(
                o32[c][:, t, :], ph[t][:].indirect(piece(n5_t, c)), pg[t][:, c * W : (c + 1) * W], ADD
            )

        def hand_on(c):
            cols = slice(c * W, (c + 1) * W)
            nc.vector.quantize_mx(
                out=ow[c][:].bitcast(FP8X4), scales=osc[:, cols], in_=o16[c][:].rearrange("p c t -> p (c t)")
            )
            nc.sync.dma_start(out_words[:, cols], ow[c][:].bitcast(I32))

        for c in range(chunks - 1):
            for t in range(PACK):
                fold_out(c, t)
                if c > 0 and t == PACK - 2:
                    hand_on(c - 1)
            nc.sync.dma_start(out_rows[:, :, c * W : (c + 1) * W], o32[c])
            nc.scalar.copy(o16[c][:], o32[c].rearrange("p t c -> p c t"))
        c = chunks - 1
        for t in range(LAST):
            fold_out(c, t)
        nc.sync.dma_start(out_rows[:, :LAST, c * W :], o32[c][:, :LAST, :])
        fold_out(c, LAST)
        nc.sync.dma_start(out_rows[:, LAST, c * W :], o32[c][:, LAST, :])
        hand_on(c - 1)
        planes = o32[c].rearrange("p t c -> p c t")
        nc.scalar.copy(o16[c][:, : W // 4, :], planes[:, : W // 4, :])
        nc.vector.tensor_copy(o16[c][:, W // 2 :, :], planes[:, W // 2 :, :])
        nc.vector.tensor_copy(o16[c][:, W // 4 : W // 2, :], planes[:, W // 4 : W // 2, :])
        for a in (W // 2, 0):
            nc.vector.quantize_mx(
                out=ow[c][:, a : a + P].bitcast(FP8X4),
                scales=osc[:, c * W + a : c * W + a + P],
                in_=o16[c][:, a : a + P, :].rearrange("p c t -> p (c t)"),
            )
        nc.sync.dma_start(out_words[:, c * W :], ow[c][:].bitcast(I32))
        for q in range(4):
            queue = nc.scalar if q % 2 == 0 else nc.sync
            queue.dma_start(out_scales[4 * q : 4 * q + 4, :], osc[:].bitcast(I32)[32 * q : 32 * q + 4, :])
